import numpy as np
import ml_dtypes


def mxq(x, axis, fmt="e4m3"):
    dtype, down = {"e4m3": (ml_dtypes.float8_e4m3fn, 7), "e5m2": (ml_dtypes.float8_e5m2, 14)}[fmt]
    v = np.moveaxis(np.asarray(x, np.float32).astype(ml_dtypes.bfloat16).astype(np.float64), axis, -1)
    blocks = v.reshape(v.shape[:-1] + (-1, 32))
    amax = np.abs(blocks).max(-1, keepdims=True)
    byte = np.maximum(np.where(amax > 0, np.frexp(amax)[1] - 1 + 127, 0) - down, 1)
    scale = np.exp2(byte - 127.0)
    codes = (blocks / scale).astype(np.float32).astype(dtype).astype(np.float64)
    return np.moveaxis((codes * scale).reshape(v.shape), -1, axis)


WIDE = False


def mx_kscale(k):
    if not WIDE:
        return np.ones(k)
    levels = np.array([30, -30])
    if k % 512:
        return np.exp2(np.random.permutation(np.resize(levels, k // 32))).repeat(32)
    a = np.empty((k // 512, 16))
    for p in range(k // 512):
        a[p, :8] = np.random.permutation(np.resize(levels, 8))
        for g in range(8):
            far = levels[np.abs(levels - a[p, g]) >= 10]
            a[p, g + 8] = far[np.random.randint(len(far))]
    return np.exp2(a.ravel()).repeat(32)


BF16 = ml_dtypes.bfloat16


def bf(x):
    return np.asarray(x, np.float32).astype(BF16)


def f64(x):
    return np.asarray(x).astype(np.float64)


M, T, N = 1024, 2048, 1024

MIX = 0.5
RESP = 0.8
TAIL = 0.75


def setup_inputs():
    s = mx_kscale(T)
    r = mx_kscale(T)
    heavy = np.random.standard_normal((M, T)) * np.exp(TAIL * np.random.standard_normal((M, T)))
    return {
        "v": bf(np.random.standard_normal((M, T))),
        "q_old": bf(np.random.standard_normal((M, T)) * s),
        "keep": bf(MIX * (1 + 0.1 * np.random.standard_normal(T))),
        "resp": bf(RESP * (1 + 0.1 * np.random.standard_normal(T)) * s),
        "e_norm": bf(heavy * r),
        "g_single": bf(np.random.standard_normal((T, N)) / np.sqrt(T) / s[:, None]),
        "g_double": bf(np.random.standard_normal((T, N)) / np.sqrt(T) / r[:, None]),
        "f_eps": bf(np.random.uniform(0.5, 1.0, M)),
    }


def reference(v, q_old, keep, resp, e_norm, g_single, g_double, f_eps):
    q = f64(keep) * f64(q_old) - f64(resp) * f64(v)
    single = mxq(q, 1, "e4m3") @ mxq(f64(g_single), 0, "e4m3")
    double = mxq(f64(e_norm), 1, "e5m2") @ mxq(f64(g_double), 0, "e4m3")
    return f64(f_eps)[:, None] * (single + double)

@@ -1,0 +1,394 @@
+from contextlib import ExitStack
+
+import concourse.mybir as mybir
+from concourse.masks import make_identity
+
+M, T, N = 1024, 2048, 1024
+FLOPS = 2 * 2 * M * T * N
+
+F32 = mybir.dt.float32
+BF16 = mybir.dt.bfloat16
+U32 = mybir.dt.uint32
+U8 = mybir.dt.uint8
+E4M3 = mybir.dt.float8_e4m3fn_x4
+E5M2 = mybir.dt.float8_e5m2_x4
+COPY = mybir.ActivationFunctionType.Copy
+MULT = mybir.AluOpType.mult
+SUB = mybir.AluOpType.subtract
+
+P = 128
+PACK = 4
+K_PASS = P * PACK
+PASSES = T // K_PASS
+ROW_TILES = M // P
+GROUP = 4
+WIDTH = GROUP * P
+N_TILE = 512
+RUN = 4
+
+SMALL_RAW = 18
+PRODUCT_BUFS = 4
+GROUPED_BUFS = 6
+RESULT_BUFS = 6
+SHARES_HEAD = (0, 256, 256)
+SHARES_FIRST = (336, 352, 336)
+SHARES_SECOND = (128, 0, 128)
+VECTOR_COLS_LAST = 288
+ORDER = ("v", "q", "gq", "e", "ge")
+WIDE = (6,)
+FIRST_STEPS = 4
+TAIL_CHUNKS = 3
+CATCH_UP = 2
+LATE_AT = (1, 1, 1)
+
+
+def tile_continuum_reaction_field_s2_kernel(
+    tc, v, q_old, keep, resp, e_norm, g_single, g_double, f_eps, out
+):
+    nc = tc.nc
+    acts = {
+        "v": v.rearrange("(p j) k -> p j k", j=ROW_TILES),
+        "q": q_old.rearrange("(p j) k -> p j k", j=ROW_TILES),
+        "e": e_norm.rearrange("(p j) k -> p j k", j=ROW_TILES),
+    }
+    kernels = {"q": g_single, "e": g_double}
+    out_rows = out.rearrange("(p j) n -> p j n", j=ROW_TILES)
+
+    with ExitStack() as ctx:
+        sb = ctx.enter_context(tc.tile_pool(name="sb", bufs=1))
+        ps = ctx.enter_context(tc.psum_pool(name="ps", bufs=1))
+
+        def tiles(name, count, shape, dtype):
+            return [sb.tile(shape, dtype, name="%s%d" % (name, i), align_bytes=64) for i in range(count)]
+
+        banks = [ps.tile([P, N_TILE], F32, name="bank%d" % i) for i in range(8)]
+        turn_banks, sum_banks = banks[:4], banks[4:]
+        ident = sb.tile([P, P], F32, name="ident")
+        keep_bf = sb.tile([P, PASSES, PACK], BF16, name="keep_bf")
+        resp_bf = sb.tile([P, PASSES, PACK], BF16, name="resp_bf")
+        feps_bf = sb.tile([P, ROW_TILES], BF16, name="feps_bf")
+        keep_f = sb.tile([P, PASSES, PACK], F32, name="keep_f")
+        resp_f = sb.tile([P, PASSES, PACK], F32, name="resp_f")
+        feps_f = sb.tile([P, ROW_TILES], F32, name="feps_f")
+        warm = sb.tile([P, 1], F32, name="warm")
+        small_raw = tiles("small_raw", SMALL_RAW, [P, PACK, K_PASS], BF16)
+        wide_raw = {a: tiles("wide_raw_" + a, 1, [P, GROUP, 2 * K_PASS], BF16) for a in acts}
+        products = tiles("product", PRODUCT_BUFS, [P, WIDTH], F32)
+        q_slots = tiles("q_slots", 2, [P, PACK, WIDTH], BF16)
+        grouped_bufs = tiles("grouped", GROUPED_BUFS, [P, PACK * WIDTH], BF16)
+        results = tiles("result", RESULT_BUFS, [P, N_TILE], F32)
+        act_codes = {a: tiles("codes_" + a, 2 * PASSES, [P, WIDTH], U32) for a in kernels}
+        act_scales = {a: tiles("scales_" + a, 2 * PASSES, [P, WIDTH], U8) for a in kernels}
+        g_codes = {a: tiles("g_codes_" + a, 2 * PASSES, [P, N_TILE], U32) for a in kernels}
+        g_scales = {a: tiles("g_scales_" + a, 2 * PASSES, [P, N_TILE], U8) for a in kernels}
+
+        used = {"small": 0, "turn": 0, "product": 0, "grouped": 0, "result": 0}
+
+        def take(kind, ring):
+            used[kind] = used[kind] + 1
+            return ring[(used[kind] - 1) % len(ring)]
+
+        act_raw = {}
+        g_raw = {}
+        turned = {}
+        product_of = {}
+        grouped_of = {}
+        result_of = {}
+
+        def load_act(a, step, count):
+            half, g = divmod(step, PASSES)
+            if count == 1:
+                raw = take("small", small_raw)
+            else:
+                raw = wide_raw[a][0]
+            src = acts[a][:, GROUP * half : GROUP * (half + 1), K_PASS * g : K_PASS * (g + count)]
+            nc.sync.dma_start(out=raw[:], in_=src)
+            for i in range(count):
+                act_raw[a, step + i] = (raw, K_PASS * i)
+
+        def load_g(a, chunk):
+            n_half, g = divmod(chunk, PASSES)
+            raw = take("small", small_raw)
+            src = kernels[a][K_PASS * g : K_PASS * (g + 1), N_TILE * n_half : N_TILE * (n_half + 1)]
+            nc.sync.dma_start(out=raw[:], in_=src.rearrange("(p t) n -> p t n", t=PACK))
+            g_raw[a, chunk] = raw
+
+        def words(a, step, j, u):
+            raw, k0 = act_raw[a, step]
+            return raw[:, j, k0 : k0 + K_PASS].bitcast(F32)[:, u : K_PASS // 2 : 2]
+
+        def turn_charges(step, u):
+            for a in ("v", "q"):
+                bank = take("turn", turn_banks)
+                turned[a, step, u] = bank
+                for j in range(GROUP):
+                    nc.tensor.transpose(bank[:, P * j : P * (j + 1)], words(a, step, j, u), ident[:])
+
+        def turn_fields(step, u):
+            bank = take("turn", turn_banks)
+            turned["e", step, u] = bank
+            for jj in range(2):
+                for w in range(2):
+                    c0 = 2 * P * w + P * jj
+                    nc.tensor.transpose(bank[:, c0 : c0 + P], words("e", step, 2 * u + jj, w), ident[:])
+
+        def slot_view(bank, e):
+            return bank[:].bitcast(BF16)[:, e : 2 * WIDTH : 2]
+
+        def response(step, u):
+            g = step % PASSES
+            for e in range(2):
+                t = 2 * u + e
+                product = take("product", products)
+                product_of[step, t] = product
+                nc.scalar.activation(
+                    out=product[:], in_=slot_view(turned["v", step, u], e), func=COPY, scale=resp_f[:, g, t : t + 1]
+                )
+
+        def charges(step, u):
+            g = step % PASSES
+            for e in range(2):
+                t = 2 * u + e
+                nc.vector.scalar_tensor_tensor(
+                    out=q_slots[step % 2][:, t, :],
+                    in0=slot_view(turned["q", step, u], e),
+                    scalar=keep_f[:, g, t : t + 1],
+                    in1=product_of[step, t][:],
+                    op0=MULT,
+                    op1=SUB,
+                )
+
+        def grouped_tile(key):
+            if key not in grouped_of:
+                grouped_of[key] = take("grouped", grouped_bufs)
+            return grouped_of[key]
+
+        def copy_fields(step, u):
+            dst = grouped_tile(("e", step))[:].bitcast(F32)[:, WIDTH * u : WIDTH * (u + 1)]
+            nc.scalar.copy(
+                out=dst.rearrange("p (r w) -> p r w", w=2),
+                in_=turned["e", step, u][:].rearrange("p (w r) -> p r w", w=2),
+            )
+
+        def interleave(copy, key, rows, c0, c1):
+            if c0 == c1:
+                return
+            dst = grouped_tile(key)[:, PACK * c0 : PACK * c1]
+            copy(
+                out=dst.rearrange("p (c i t) -> p c t i", i=RUN, t=PACK),
+                in_=rows[:, :, c0:c1].rearrange("p t (c i) -> p c t i", i=RUN),
+            )
+
+        def group_q(step):
+            interleave(nc.vector.tensor_copy, ("q", step), q_slots[step % 2], 0, WIDTH)
+
+        def group_g(copy, a, chunk, c0, c1):
+            interleave(copy, ("g", a, chunk), g_raw[a, chunk], c0, c1)
+
+        def quantize_act(a, step):
+            nc.vector.quantize_mx(
+                out=act_codes[a][step][:].bitcast(E4M3 if a == "q" else E5M2),
+                scales=act_scales[a][step][:],
+                in_=grouped_of[a, step][:],
+            )
+
+        def quantize_g(a, chunk):
+            nc.vector.quantize_mx(
+                out=g_codes[a][chunk][:].bitcast(E4M3),
+                scales=g_scales[a][chunk][:],
+                in_=grouped_of["g", a, chunk][:],
+            )
+
+        def multiply(bank, a, half, j, n_half, g):
+            step = PASSES * half + g
+            chunk = PASSES * n_half + g
+            cols = slice(P * j, P * (j + 1))
+            nc.tensor.matmul_mx(
+                out=bank[:],
+                lhsT=act_codes[a][step][:, cols].bitcast(E4M3 if a == "q" else E5M2),
+                lhsT_scale=act_scales[a][step][:, cols],
+                rhs=g_codes[a][chunk][:].bitcast(E4M3),
+                rhs_scale=g_scales[a][chunk][:],
+                start=(a == "q" and g == 0),
+                stop=(a == "e" and g == PASSES - 1),
+            )
+
+        def multiply_group(ring, a, half, n_half, g):
+            for j in range(GROUP):
+                multiply(ring[j], a, half, j, n_half, g)
+
+        def finish(bank, half, j, n_half):
+            tile_row = GROUP * half + j
+            result = take("result", results)
+            result_of[tile_row, n_half] = result
+            factor = feps_f[:, tile_row : tile_row + 1]
+            if j % 2 == 0:
+                nc.scalar.activation(out=result[:], in_=bank[:], func=COPY, scale=factor)
+            else:
+                nc.vector.tensor_scalar(out=result[:], in0=bank[:], scalar1=factor, scalar2=None, op0=MULT)
+
+        def store(half, j, n_half):
+            tile_row = GROUP * half + j
+            nc.sync.dma_start(
+                out=out_rows[:, tile_row, N_TILE * n_half : N_TILE * (n_half + 1)], in_=result_of[tile_row, n_half][:]
+            )
+
+        s_copy, v_copy = nc.scalar.copy, nc.vector.tensor_copy
+        steps = 2 * PASSES
+        chunks = [(a, chunk) for chunk in range(2 * PASSES) for a in ("q", "e")]
+        late = chunks[2 * PASSES :]
+        stream = {"grouped": 0, "quantized": 0}
+
+        def group_stream(copy, cols):
+            end = min(stream["grouped"] + cols, len(chunks) * N_TILE)
+            while stream["grouped"] < end:
+                i, c0 = divmod(stream["grouped"], N_TILE)
+                c1 = min(N_TILE, end - i * N_TILE)
+                group_g(copy, *chunks[i], c0, c1)
+                stream["grouped"] = i * N_TILE + c1
+
+        def quantize_stream(cols):
+            while (stream["quantized"] + 1) * N_TILE <= cols:
+                quantize_g(*chunks[stream["quantized"]])
+                stream["quantized"] = stream["quantized"] + 1
+
+        def multiply_late(bank, half, j, items):
+            for a, chunk in items:
+                multiply(bank, a, half, j, 1, chunk - PASSES)
+
+        def multiply_step(a, step):
+            if step >= 0:
+                multiply_group(sum_banks, a, step // PASSES, 0, step % PASSES)
+
+        loads = []
+        nl = 0
+        for step in range(steps):
+            for a in ORDER:
+                if a in acts:
+                    if step in WIDE:
+                        loads.append(("act", a, step, 2))
+                    elif step - 1 not in WIDE:
+                        loads.append(("act", a, step, 1))
+                elif step < PASSES:
+                    loads.append(("g", a[1], step, 1))
+            if PASSES <= step < steps - 1:
+                for i in range(LATE_AT[step - PASSES]):
+                    loads.append(("g",) + late[nl] + (1,))
+                    nl = nl + 1
+        for item in late[nl:]:
+            loads.append(("g",) + item + (1,))
+        issued = {"n": 0}
+        holder = {}
+
+        def issue_loads(turned_steps, fields_steps):
+            while issued["n"] < len(loads):
+                kind, a, idx, count = loads[issued["n"]]
+                slot = ("small", used["small"] % SMALL_RAW) if count == 1 else ("wide", a)
+                if slot in holder:
+                    hk, ha, hi = holder[slot]
+                    if hk == "act" and hi >= (fields_steps if ha == "e" else turned_steps):
+                        return
+                    if hk == "g" and (chunks.index((ha, hi)) + 1) * N_TILE > stream["grouped"]:
+                        return
+                holder[slot] = (kind, a, idx + count - 1)
+                if kind == "act":
+                    load_act(a, idx, count)
+                else:
+                    load_g(a, idx)
+                issued["n"] = issued["n"] + 1
+
+        with tc.manual_schedule():
+            nc.scalar.dma_start(out=resp_bf[:], in_=resp.rearrange("(g p t) -> p g t", p=P, t=PACK))
+            nc.scalar.dma_start(out=keep_bf[:], in_=keep.rearrange("(g p t) -> p g t", p=P, t=PACK))
+            nc.scalar.dma_start(out=feps_bf[:], in_=f_eps.rearrange("(p j) -> p j", j=ROW_TILES))
+            make_identity(nc, ident[:])
+            nc.scalar.activation(out=warm[:], in_=ident[:, 0:1], func=COPY)
+            issue_loads(0, 0)
+            nc.vector.tensor_copy(out=resp_f[:], in_=resp_bf[:])
+            nc.vector.tensor_copy(out=keep_f[:], in_=keep_bf[:])
+            nc.vector.tensor_copy(out=feps_f[:], in_=feps_bf[:])
+
+            for step in range(steps):
+                prev = step - 1
+                shares = SHARES_HEAD if step == 0 else SHARES_FIRST if step <= FIRST_STEPS else SHARES_SECOND
+                done_before = stream["grouped"]
+                turn_charges(step, 0)
+                if step > 0:
+                    turn_fields(prev, 1)
+                    group_q(prev)
+                multiply_step("e", step - 2)
+                response(step, 0)
+                if step > 0:
+                    copy_fields(prev, 1)
+                charges(step, 0)
+                if step == PASSES + 1:
+                    for j in range(GROUP):
+                        finish(sum_banks[j], 0, j, 0)
+                if step > 0:
+                    quantize_act("q", prev)
+                group_stream(s_copy, shares[0])
+                quantize_stream(done_before)
+                group_stream(v_copy, shares[1])
+                if step > 0:
+                    quantize_act("e", prev)
+                turn_charges(step, 1)
+                turn_fields(step, 0)
+                multiply_step("q", prev)
+                response(step, 1)
+                copy_fields(step, 0)
+                charges(step, 1)
+                quantize_stream(stream["grouped"])
+                group_stream(s_copy, shares[2])
+                issue_loads(step + 1, step)
+            assert issued["n"] == len(loads)
+            for j in range(GROUP):
+                store(0, j, 0)
+
+            last = steps - 1
+            turn_fields(last, 1)
+            group_q(last)
+            multiply_step("e", last - 1)
+            copy_fields(last, 1)
+            free_order = [turn_banks[(used["turn"] + i) % len(turn_banks)] for i in range(GROUP)]
+            count = stream["quantized"] - 2 * PASSES
+            early = late[:count]
+            done_before = stream["grouped"]
+            group_stream(s_copy, -stream["grouped"] % N_TILE)
+            quantize_stream(done_before)
+            quantize_act("q", last)
+            quantize_act("e", last)
+            for j in range(GROUP // 2):
+                multiply_late(free_order[j], 0, j, early)
+            multiply_step("q", last)
+            multiply_late(free_order[2], 0, 2, early)
+            multiply_step("e", last)
+            multiply_late(free_order[3], 0, 3, early)
+            done_before = stream["grouped"]
+            group_stream(s_copy, N_TILE - VECTOR_COLS_LAST)
+            group_stream(v_copy, VECTOR_COLS_LAST)
+            quantize_stream(done_before)
+            for j in range(GROUP):
+                finish(sum_banks[j], 1, j, 0)
+                store(1, j, 0)
+            while stream["quantized"] < len(chunks):
+                done_before = stream["grouped"]
+                group_stream(s_copy, N_TILE - VECTOR_COLS_LAST)
+                group_stream(v_copy, VECTOR_COLS_LAST)
+                quantize_stream(done_before)
+            shared = len(late) - TAIL_CHUNKS
+            rest = late[shared:]
+            behind = 0
+            for i in range(count, shared):
+                for j in range(GROUP):
+                    multiply_late(free_order[j], 0, j, [late[i]])
+                upto = min(behind + CATCH_UP, i + 1)
+                for j in range(GROUP):
+                    multiply_late(sum_banks[j], 1, j, late[behind:upto])
+                behind = upto
+            for j in range(GROUP):
+                multiply_late(sum_banks[j], 1, j, late[behind:shared])
+            for half, ring in enumerate((free_order, sum_banks)):
+                for j in range(GROUP):
+                    multiply_late(ring[j], half, j, rest)
+                    finish(ring[j], half, j, 1)
+                    store(half, j, 1)

@@ -15,6 +15,7 @@ E5M2 = mybir.dt.float8_e5m2_x4
 COPY = mybir.ActivationFunctionType.Copy
 MULT = mybir.AluOpType.mult
 SUB = mybir.AluOpType.subtract
+ADD = mybir.AluOpType.add
 
 P = 128
 PACK = 4
@@ -23,35 +24,31 @@ PASSES = T // K_PASS
 ROW_TILES = M // P
 GROUP = 4
 WIDTH = GROUP * P
+STEPS = PASSES * ROW_TILES // GROUP
 N_TILE = 512
 RUN = 4
 
-SMALL_RAW = 18
+RAW_BUFS = 24
 PRODUCT_BUFS = 4
-GROUPED_BUFS = 6
+GROUPED_BUFS = 5
 RESULT_BUFS = 6
-SHARES_HEAD = (0, 256, 256)
-SHARES_FIRST = (336, 352, 336)
-SHARES_SECOND = (128, 0, 128)
-VECTOR_COLS_LAST = 288
-ORDER = ("v", "q", "gq", "e", "ge")
-WIDE = (6,)
-FIRST_STEPS = 4
-TAIL_CHUNKS = 3
-CATCH_UP = 2
-LATE_AT = (1, 1, 1)
+POOL_COLS = 160
+VECTOR_COLS = 64
+VECTOR_COLS_END = 288
+END_CHUNKS = 3
 
 
 def tile_continuum_reaction_field_s2_kernel(
     tc, v, q_old, keep, resp, e_norm, g_single, g_double, f_eps, out
 ):
     nc = tc.nc
-    acts = {
+    rows_of = {
         "v": v.rearrange("(p j) k -> p j k", j=ROW_TILES),
         "q": q_old.rearrange("(p j) k -> p j k", j=ROW_TILES),
         "e": e_norm.rearrange("(p j) k -> p j k", j=ROW_TILES),
     }
-    kernels = {"q": g_single, "e": g_double}
+    green = {"q": g_single, "e": g_double}
+    row_format = {"q": E4M3, "e": E5M2}
     out_rows = out.rearrange("(p j) n -> p j n", j=ROW_TILES)
 
     with ExitStack() as ctx:
@@ -62,166 +59,152 @@ def tile_continuum_reaction_field_s2_kernel(
             return [sb.tile(shape, dtype, name="%s%d" % (name, i), align_bytes=64) for i in range(count)]
 
         banks = [ps.tile([P, N_TILE], F32, name="bank%d" % i) for i in range(8)]
-        turn_banks, sum_banks = banks[:4], banks[4:]
+        turn_banks, sum_banks = banks[:GROUP], banks[GROUP:]
         ident = sb.tile([P, P], F32, name="ident")
-        keep_bf = sb.tile([P, PASSES, PACK], BF16, name="keep_bf")
-        resp_bf = sb.tile([P, PASSES, PACK], BF16, name="resp_bf")
+        coef_rows = sb.tile([P, K_PASS], BF16, name="coef_rows")
+        coef = sb.tile([P, 2, 4 * PASSES], F32, name="coef")
         feps_bf = sb.tile([P, ROW_TILES], BF16, name="feps_bf")
-        keep_f = sb.tile([P, PASSES, PACK], F32, name="keep_f")
-        resp_f = sb.tile([P, PASSES, PACK], F32, name="resp_f")
-        feps_f = sb.tile([P, ROW_TILES], F32, name="feps_f")
+        feps = sb.tile([P, ROW_TILES], F32, name="feps")
         warm = sb.tile([P, 1], F32, name="warm")
-        small_raw = tiles("small_raw", SMALL_RAW, [P, PACK, K_PASS], BF16)
-        wide_raw = {a: tiles("wide_raw_" + a, 1, [P, GROUP, 2 * K_PASS], BF16) for a in acts}
+        raw_bufs = tiles("raw", RAW_BUFS, [P, PACK, K_PASS], BF16)
         products = tiles("product", PRODUCT_BUFS, [P, WIDTH], F32)
         q_slots = tiles("q_slots", 2, [P, PACK, WIDTH], BF16)
         grouped_bufs = tiles("grouped", GROUPED_BUFS, [P, PACK * WIDTH], BF16)
+        shared_grouped = sb.tile([P, PACK * N_TILE], BF16, name="shared_grouped", align_bytes=64)
         results = tiles("result", RESULT_BUFS, [P, N_TILE], F32)
-        act_codes = {a: tiles("codes_" + a, 2 * PASSES, [P, WIDTH], U32) for a in kernels}
-        act_scales = {a: tiles("scales_" + a, 2 * PASSES, [P, WIDTH], U8) for a in kernels}
-        g_codes = {a: tiles("g_codes_" + a, 2 * PASSES, [P, N_TILE], U32) for a in kernels}
-        g_scales = {a: tiles("g_scales_" + a, 2 * PASSES, [P, N_TILE], U8) for a in kernels}
+        row_codes = {a: tiles("row_codes_" + a, STEPS, [P, WIDTH], U32) for a in green}
+        row_scales = {a: tiles("row_scales_" + a, STEPS, [P, WIDTH], U8) for a in green}
+        g_codes = {a: tiles("g_codes_" + a, 2 * PASSES, [P, N_TILE], U32) for a in green}
+        g_scales = {a: tiles("g_scales_" + a, 2 * PASSES, [P, N_TILE], U8) for a in green}
 
-        used = {"small": 0, "turn": 0, "product": 0, "grouped": 0, "result": 0}
+        taken = {"raw": 0, "turn": 0, "product": 0, "grouped": 0, "result": 0}
+        raw_of, turned, product_of, grouped_of, result_of = {}, {}, {}, {}, {}
 
         def take(kind, ring):
-            used[kind] = used[kind] + 1
-            return ring[(used[kind] - 1) % len(ring)]
+            taken[kind] = taken[kind] + 1
+            return ring[(taken[kind] - 1) % len(ring)]
 
-        act_raw = {}
-        g_raw = {}
-        turned = {}
-        product_of = {}
-        grouped_of = {}
-        result_of = {}
-
-        def load_act(a, step, count):
-            half, g = divmod(step, PASSES)
-            if count == 1:
-                raw = take("small", small_raw)
+        def load(kind, a, index):
+            raw = take("raw", raw_bufs)
+            raw_of[kind, a, index] = raw
+            half, g = divmod(index, PASSES)
+            k_range = slice(K_PASS * g, K_PASS * (g + 1))
+            if kind == "rows":
+                src = rows_of[a][:, GROUP * half : GROUP * (half + 1), k_range]
             else:
-                raw = wide_raw[a][0]
-            src = acts[a][:, GROUP * half : GROUP * (half + 1), K_PASS * g : K_PASS * (g + count)]
+                src = green[a][k_range, N_TILE * half : N_TILE * (half + 1)].rearrange("(p t) n -> p t n", t=PACK)
             nc.sync.dma_start(out=raw[:], in_=src)
-            for i in range(count):
-                act_raw[a, step + i] = (raw, K_PASS * i)
 
-        def load_g(a, chunk):
-            n_half, g = divmod(chunk, PASSES)
-            raw = take("small", small_raw)
-            src = kernels[a][K_PASS * g : K_PASS * (g + 1), N_TILE * n_half : N_TILE * (n_half + 1)]
-            nc.sync.dma_start(out=raw[:], in_=src.rearrange("(p t) n -> p t n", t=PACK))
-            g_raw[a, chunk] = raw
-
-        def words(a, step, j, u):
-            raw, k0 = act_raw[a, step]
-            return raw[:, j, k0 : k0 + K_PASS].bitcast(F32)[:, u : K_PASS // 2 : 2]
+        def every_second_word(row, u):
+            return row.bitcast(F32)[:, u : K_PASS // 2 : 2]
 
         def turn_charges(step, u):
             for a in ("v", "q"):
                 bank = take("turn", turn_banks)
                 turned[a, step, u] = bank
                 for j in range(GROUP):
-                    nc.tensor.transpose(bank[:, P * j : P * (j + 1)], words(a, step, j, u), ident[:])
+                    src = every_second_word(raw_of["rows", a, step][:, j, :], u)
+                    nc.tensor.transpose(bank[:, P * j : P * (j + 1)], src, ident[:])
 
-        def turn_fields(step, u):
+        def turn_fields(step, pair):
             bank = take("turn", turn_banks)
-            turned["e", step, u] = bank
+            turned["e", step, pair] = bank
             for jj in range(2):
-                for w in range(2):
-                    c0 = 2 * P * w + P * jj
-                    nc.tensor.transpose(bank[:, c0 : c0 + P], words("e", step, 2 * u + jj, w), ident[:])
+                for u in range(2):
+                    src = every_second_word(raw_of["rows", "e", step][:, 2 * pair + jj, :], u)
+                    c0 = P * (2 * u + jj)
+                    nc.tensor.transpose(bank[:, c0 : c0 + P], src, ident[:])
 
-        def slot_view(bank, e):
+        def half_words(bank, e):
             return bank[:].bitcast(BF16)[:, e : 2 * WIDTH : 2]
 
         def response(step, u):
-            g = step % PASSES
             for e in range(2):
-                t = 2 * u + e
                 product = take("product", products)
-                product_of[step, t] = product
+                product_of[step, u, e] = product
+                c = 2 * (PASSES + step % PASSES) + e
                 nc.scalar.activation(
-                    out=product[:], in_=slot_view(turned["v", step, u], e), func=COPY, scale=resp_f[:, g, t : t + 1]
+                    out=product[:], in_=half_words(turned["v", step, u], e), func=COPY, scale=coef[:, u, c : c + 1]
                 )
 
         def charges(step, u):
-            g = step % PASSES
             for e in range(2):
-                t = 2 * u + e
+                c = 2 * (step % PASSES) + e
                 nc.vector.scalar_tensor_tensor(
-                    out=q_slots[step % 2][:, t, :],
-                    in0=slot_view(turned["q", step, u], e),
-                    scalar=keep_f[:, g, t : t + 1],
-                    in1=product_of[step, t][:],
+                    out=q_slots[step % 2][:, 2 * u + e, :],
+                    in0=half_words(turned["q", step, u], e),
+                    scalar=coef[:, u, c : c + 1],
+                    in1=product_of[step, u, e][:],
                     op0=MULT,
                     op1=SUB,
                 )
 
-        def grouped_tile(key):
-            if key not in grouped_of:
-                grouped_of[key] = take("grouped", grouped_bufs)
-            return grouped_of[key]
-
-        def copy_fields(step, u):
-            dst = grouped_tile(("e", step))[:].bitcast(F32)[:, WIDTH * u : WIDTH * (u + 1)]
+        def copy_fields(step, pair):
+            if pair == 0:
+                grouped_of["rows", "e", step] = take("grouped", grouped_bufs)
+            dst = grouped_of["rows", "e", step][:].bitcast(F32)[:, WIDTH * pair : WIDTH * (pair + 1)]
             nc.scalar.copy(
-                out=dst.rearrange("p (r w) -> p r w", w=2),
-                in_=turned["e", step, u][:].rearrange("p (w r) -> p r w", w=2),
+                out=dst.rearrange("p (r u) -> p r u", u=2),
+                in_=turned["e", step, pair][:].rearrange("p (u r) -> p r u", u=2),
             )
 
-        def interleave(copy, key, rows, c0, c1):
-            if c0 == c1:
-                return
-            dst = grouped_tile(key)[:, PACK * c0 : PACK * c1]
+        def interleave(copy, grouped, slots, c0, c1):
             copy(
-                out=dst.rearrange("p (c i t) -> p c t i", i=RUN, t=PACK),
-                in_=rows[:, :, c0:c1].rearrange("p t (c i) -> p c t i", i=RUN),
+                out=grouped[:, PACK * c0 : PACK * c1].rearrange("p (c i t) -> p c t i", i=RUN, t=PACK),
+                in_=slots[:, :, c0:c1].rearrange("p t (c i) -> p c t i", i=RUN),
             )
 
-        def group_q(step):
-            interleave(nc.vector.tensor_copy, ("q", step), q_slots[step % 2], 0, WIDTH)
+        def group_charges(step):
+            grouped_of["rows", "q", step] = take("grouped", grouped_bufs)
+            interleave(nc.vector.tensor_copy, grouped_of["rows", "q", step], q_slots[step % 2], 0, WIDTH)
 
-        def group_g(copy, a, chunk, c0, c1):
-            interleave(copy, ("g", a, chunk), g_raw[a, chunk], c0, c1)
-
-        def quantize_act(a, step):
-            nc.vector.quantize_mx(
-                out=act_codes[a][step][:].bitcast(E4M3 if a == "q" else E5M2),
-                scales=act_scales[a][step][:],
-                in_=grouped_of[a, step][:],
+        def group_on_pool(item):
+            grouped_of[item] = shared_grouped
+            nc.gpsimd.tensor_scalar(
+                out=shared_grouped[:, 0 : PACK * POOL_COLS].rearrange("p (c t) -> p c t", t=PACK),
+                in0=raw_of[item][:, :, 0:POOL_COLS].rearrange("p t c -> p c t"),
+                scalar1=1.0,
+                scalar2=0.0,
+                op0=MULT,
+                op1=ADD,
             )
 
-        def quantize_g(a, chunk):
-            nc.vector.quantize_mx(
-                out=g_codes[a][chunk][:].bitcast(E4M3),
-                scales=g_scales[a][chunk][:],
-                in_=grouped_of["g", a, chunk][:],
-            )
+        def quantize(item):
+            kind, a, index = item
+            if kind == "rows":
+                codes, scales = row_codes[a][index][:].bitcast(row_format[a]), row_scales[a][index]
+            else:
+                codes, scales = g_codes[a][index][:].bitcast(E4M3), g_scales[a][index]
+            nc.vector.quantize_mx(out=codes, scales=scales[:], in_=grouped_of[item][:])
 
-        def multiply(bank, a, half, j, n_half, g):
+        def multiply(bank, half, j, item):
+            a, chunk = item[1:]
+            g = chunk % PASSES
             step = PASSES * half + g
-            chunk = PASSES * n_half + g
             cols = slice(P * j, P * (j + 1))
             nc.tensor.matmul_mx(
                 out=bank[:],
-                lhsT=act_codes[a][step][:, cols].bitcast(E4M3 if a == "q" else E5M2),
-                lhsT_scale=act_scales[a][step][:, cols],
+                lhsT=row_codes[a][step][:, cols].bitcast(row_format[a]),
+                lhsT_scale=row_scales[a][step][:, cols],
                 rhs=g_codes[a][chunk][:].bitcast(E4M3),
                 rhs_scale=g_scales[a][chunk][:],
                 start=(a == "q" and g == 0),
                 stop=(a == "e" and g == PASSES - 1),
             )
 
-        def multiply_group(ring, a, half, n_half, g):
-            for j in range(GROUP):
-                multiply(ring[j], a, half, j, n_half, g)
+        def multiply_tiles(ring, half, tile_range, items):
+            for j in tile_range:
+                for item in items:
+                    multiply(ring[j], half, j, item)
+
+        def multiply_step(a, step):
+            multiply_tiles(sum_banks, step // PASSES, range(GROUP), [("g", a, step % PASSES)])
 
         def finish(bank, half, j, n_half):
             tile_row = GROUP * half + j
             result = take("result", results)
             result_of[tile_row, n_half] = result
-            factor = feps_f[:, tile_row : tile_row + 1]
+            factor = feps[:, tile_row : tile_row + 1]
             if j % 2 == 0:
                 nc.scalar.activation(out=result[:], in_=bank[:], func=COPY, scale=factor)
             else:
@@ -229,166 +212,128 @@ def tile_continuum_reaction_field_s2_kernel(
 
         def store(half, j, n_half):
             tile_row = GROUP * half + j
-            nc.sync.dma_start(
-                out=out_rows[:, tile_row, N_TILE * n_half : N_TILE * (n_half + 1)], in_=result_of[tile_row, n_half][:]
-            )
+            dst = out_rows[:, tile_row, N_TILE * n_half : N_TILE * (n_half + 1)]
+            nc.sync.dma_start(out=dst, in_=result_of[tile_row, n_half][:])
 
-        s_copy, v_copy = nc.scalar.copy, nc.vector.tensor_copy
-        steps = 2 * PASSES
-        chunks = [(a, chunk) for chunk in range(2 * PASSES) for a in ("q", "e")]
-        late = chunks[2 * PASSES :]
-        stream = {"grouped": 0, "quantized": 0}
+        late = [("g", a, PASSES + g) for g in range(PASSES) for a in ("q", "e")]
+        window = {step: (("g", "q", step - 1), ("g", "e", step - 1)) for step in range(1, PASSES + 1)}
+        window[STEPS - 1] = (late[0], late[1])
 
-        def group_stream(copy, cols):
-            end = min(stream["grouped"] + cols, len(chunks) * N_TILE)
-            while stream["grouped"] < end:
-                i, c0 = divmod(stream["grouped"], N_TILE)
-                c1 = min(N_TILE, end - i * N_TILE)
-                group_g(copy, *chunks[i], c0, c1)
-                stream["grouped"] = i * N_TILE + c1
+        def step_loads(step):
+            v_rows, q_rows, e_rows = [("rows", a, step) for a in ("v", "q", "e")]
+            if 1 <= step <= PASSES:
+                return [v_rows, q_rows, window[step][0], e_rows, window[step][1]]
+            return [v_rows, q_rows, e_rows]
 
-        def quantize_stream(cols):
-            while (stream["quantized"] + 1) * N_TILE <= cols:
-                quantize_g(*chunks[stream["quantized"]])
-                stream["quantized"] = stream["quantized"] + 1
+        loads = [item for step in range(STEPS) for item in step_loads(step)] + late
 
-        def multiply_late(bank, half, j, items):
-            for a, chunk in items:
-                multiply(bank, a, half, j, 1, chunk - PASSES)
+        def issue_loads(upto):
+            for item in loads[taken["raw"] : upto]:
+                load(*item)
 
-        def multiply_step(a, step):
-            if step >= 0:
-                multiply_group(sum_banks, a, step // PASSES, 0, step % PASSES)
-
-        loads = []
-        nl = 0
-        for step in range(steps):
-            for a in ORDER:
-                if a in acts:
-                    if step in WIDE:
-                        loads.append(("act", a, step, 2))
-                    elif step - 1 not in WIDE:
-                        loads.append(("act", a, step, 1))
-                elif step < PASSES:
-                    loads.append(("g", a[1], step, 1))
-            if PASSES <= step < steps - 1:
-                for i in range(LATE_AT[step - PASSES]):
-                    loads.append(("g",) + late[nl] + (1,))
-                    nl = nl + 1
-        for item in late[nl:]:
-            loads.append(("g",) + item + (1,))
-        issued = {"n": 0}
-        holder = {}
-
-        def issue_loads(turned_steps, fields_steps):
-            while issued["n"] < len(loads):
-                kind, a, idx, count = loads[issued["n"]]
-                slot = ("small", used["small"] % SMALL_RAW) if count == 1 else ("wide", a)
-                if slot in holder:
-                    hk, ha, hi = holder[slot]
-                    if hk == "act" and hi >= (fields_steps if ha == "e" else turned_steps):
-                        return
-                    if hk == "g" and (chunks.index((ha, hi)) + 1) * N_TILE > stream["grouped"]:
-                        return
-                holder[slot] = (kind, a, idx + count - 1)
-                if kind == "act":
-                    load_act(a, idx, count)
-                else:
-                    load_g(a, idx)
-                issued["n"] = issued["n"] + 1
+        scalar_cols = (POOL_COLS, N_TILE - VECTOR_COLS)
+        vector_cols = (N_TILE - VECTOR_COLS, N_TILE)
 
         with tc.manual_schedule():
-            nc.scalar.dma_start(out=resp_bf[:], in_=resp.rearrange("(g p t) -> p g t", p=P, t=PACK))
-            nc.scalar.dma_start(out=keep_bf[:], in_=keep.rearrange("(g p t) -> p g t", p=P, t=PACK))
-            nc.scalar.dma_start(out=feps_bf[:], in_=f_eps.rearrange("(p j) -> p j", j=ROW_TILES))
+            nc.gpsimd.memset(coef_rows[:], 0.0)
+            nc.scalar.dma_start(out=coef_rows[0:PASSES, :], in_=keep.rearrange("(g k) -> g k", g=PASSES))
+            nc.scalar.dma_start(out=coef_rows[PASSES : 2 * PASSES, :], in_=resp.rearrange("(g k) -> g k", g=PASSES))
             make_identity(nc, ident[:])
             nc.scalar.activation(out=warm[:], in_=ident[:, 0:1], func=COPY)
-            issue_loads(0, 0)
-            nc.vector.tensor_copy(out=resp_f[:], in_=resp_bf[:])
-            nc.vector.tensor_copy(out=keep_f[:], in_=keep_bf[:])
-            nc.vector.tensor_copy(out=feps_f[:], in_=feps_bf[:])
+            issue_loads(len(step_loads(0)) + len(step_loads(1)))
+            nc.sync.dma_start(out=feps_bf[:], in_=f_eps.rearrange("(p j) -> p j", j=ROW_TILES))
+            issue_loads(RAW_BUFS)
+            for u in range(2):
+                nc.tensor.transpose(sum_banks[0][:, P * u : P * (u + 1)], every_second_word(coef_rows[:], u), ident[:])
+            coef_turned = sum_banks[0][:, 0 : 2 * P].bitcast(BF16).rearrange("p (u x) -> p u x", u=2)
+            nc.vector.tensor_copy(out=coef[:], in_=coef_turned[:, :, 0 : 4 * PASSES])
 
-            for step in range(steps):
+            freed = 0
+            for step in range(STEPS):
                 prev = step - 1
-                shares = SHARES_HEAD if step == 0 else SHARES_FIRST if step <= FIRST_STEPS else SHARES_SECOND
-                done_before = stream["grouped"]
                 turn_charges(step, 0)
-                if step > 0:
+                if step >= 1:
                     turn_fields(prev, 1)
-                    group_q(prev)
-                multiply_step("e", step - 2)
+                    group_charges(prev)
+                if prev in window:
+                    quantize(window[prev][1])
+                if step >= 2:
+                    multiply_step("e", step - 2)
                 response(step, 0)
-                if step > 0:
-                    copy_fields(prev, 1)
+                if step in window:
+                    group_on_pool(window[step][0])
                 charges(step, 0)
-                if step == PASSES + 1:
+                if step in window:
+                    interleave(nc.scalar.copy, shared_grouped, raw_of[window[step][0]], *scalar_cols)
+                if step >= 1:
+                    copy_fields(prev, 1)
+                if step in window:
+                    interleave(nc.vector.tensor_copy, shared_grouped, raw_of[window[step][0]], *vector_cols)
+                if step >= 1:
+                    quantize(("rows", "q", prev))
+                if step - 2 == PASSES - 1:
+                    nc.vector.tensor_copy(out=feps[:], in_=feps_bf[:])
                     for j in range(GROUP):
                         finish(sum_banks[j], 0, j, 0)
-                if step > 0:
-                    quantize_act("q", prev)
-                group_stream(s_copy, shares[0])
-                quantize_stream(done_before)
-                group_stream(v_copy, shares[1])
-                if step > 0:
-                    quantize_act("e", prev)
+                if step in window:
+                    quantize(window[step][0])
+
                 turn_charges(step, 1)
                 turn_fields(step, 0)
-                multiply_step("q", prev)
+                if step >= 1:
+                    multiply_step("q", prev)
+                    quantize(("rows", "e", prev))
                 response(step, 1)
-                copy_fields(step, 0)
+                if step in window:
+                    group_on_pool(window[step][1])
                 charges(step, 1)
-                quantize_stream(stream["grouped"])
-                group_stream(s_copy, shares[2])
-                issue_loads(step + 1, step)
-            assert issued["n"] == len(loads)
+                if step in window:
+                    interleave(nc.scalar.copy, shared_grouped, raw_of[window[step][1]], *scalar_cols)
+                copy_fields(step, 0)
+                if step in window:
+                    interleave(nc.vector.tensor_copy, shared_grouped, raw_of[window[step][1]], *vector_cols)
+                if step >= 1:
+                    freed = freed + len(step_loads(prev))
+                    issue_loads(RAW_BUFS + freed)
             for j in range(GROUP):
                 store(0, j, 0)
 
-            last = steps - 1
+            last = STEPS - 1
             turn_fields(last, 1)
-            group_q(last)
+            group_charges(last)
             multiply_step("e", last - 1)
             copy_fields(last, 1)
-            free_order = [turn_banks[(used["turn"] + i) % len(turn_banks)] for i in range(GROUP)]
-            count = stream["quantized"] - 2 * PASSES
-            early = late[:count]
-            done_before = stream["grouped"]
-            group_stream(s_copy, -stream["grouped"] % N_TILE)
-            quantize_stream(done_before)
-            quantize_act("q", last)
-            quantize_act("e", last)
-            for j in range(GROUP // 2):
-                multiply_late(free_order[j], 0, j, early)
+            quantize(late[1])
+            quantize(("rows", "q", last))
+            quantize(("rows", "e", last))
+            free_banks = [turn_banks[(taken["turn"] + i) % GROUP] for i in range(GROUP)]
+            multiply_tiles(free_banks, 0, range(GROUP // 2), late[:2])
             multiply_step("q", last)
-            multiply_late(free_order[2], 0, 2, early)
             multiply_step("e", last)
-            multiply_late(free_order[3], 0, 3, early)
-            done_before = stream["grouped"]
-            group_stream(s_copy, N_TILE - VECTOR_COLS_LAST)
-            group_stream(v_copy, VECTOR_COLS_LAST)
-            quantize_stream(done_before)
-            for j in range(GROUP):
-                finish(sum_banks[j], 1, j, 0)
-                store(1, j, 0)
-            while stream["quantized"] < len(chunks):
-                done_before = stream["grouped"]
-                group_stream(s_copy, N_TILE - VECTOR_COLS_LAST)
-                group_stream(v_copy, VECTOR_COLS_LAST)
-                quantize_stream(done_before)
-            shared = len(late) - TAIL_CHUNKS
-            rest = late[shared:]
+            multiply_tiles(free_banks, 0, range(GROUP // 2, GROUP), late[:2])
+
+            for i in range(2, len(late) + 1):
+                if i < len(late):
+                    grouped_of[late[i]] = take("grouped", grouped_bufs)
+                    split = N_TILE - VECTOR_COLS_END
+                    interleave(nc.scalar.copy, grouped_of[late[i]], raw_of[late[i]], 0, split)
+                    interleave(nc.vector.tensor_copy, grouped_of[late[i]], raw_of[late[i]], split, N_TILE)
+                if i > 2:
+                    quantize(late[i - 1])
+                if i == 3:
+                    for j in range(GROUP):
+                        finish(sum_banks[j], 1, j, 0)
+                        store(1, j, 0)
+
+            shared = len(late) - END_CHUNKS
             behind = 0
-            for i in range(count, shared):
-                for j in range(GROUP):
-                    multiply_late(free_order[j], 0, j, [late[i]])
-                upto = min(behind + CATCH_UP, i + 1)
-                for j in range(GROUP):
-                    multiply_late(sum_banks[j], 1, j, late[behind:upto])
+            for i in range(2, shared):
+                multiply_tiles(free_banks, 0, range(GROUP), [late[i]])
+                upto = min(behind + 2, i + 1)
+                multiply_tiles(sum_banks, 1, range(GROUP), late[behind:upto])
                 behind = upto
-            for j in range(GROUP):
-                multiply_late(sum_banks[j], 1, j, late[behind:shared])
-            for half, ring in enumerate((free_order, sum_banks)):
+            for half, ring in enumerate((free_banks, sum_banks)):
                 for j in range(GROUP):
-                    multiply_late(ring[j], half, j, rest)
+                    multiply_tiles(ring, half, [j], late[shared:])
                     finish(ring[j], half, j, 1)
                     store(half, j, 1)

@@ -235,11 +235,12 @@ def tile_continuum_reaction_field_s2_kernel(
         vector_cols = (N_TILE - VECTOR_COLS, N_TILE)
 
         with tc.manual_schedule():
-            nc.gpsimd.memset(coef_rows[:], 0.0)
-            nc.scalar.dma_start(out=coef_rows[0:PASSES, :], in_=keep.rearrange("(g k) -> g k", g=PASSES))
-            nc.scalar.dma_start(out=coef_rows[PASSES : 2 * PASSES, :], in_=resp.rearrange("(g k) -> g k", g=PASSES))
+            nc.vector.memset(coef_rows[:], 0.0)
             make_identity(nc, ident[:])
             nc.scalar.activation(out=warm[:], in_=ident[:, 0:1], func=COPY)
+            issue_loads(1)
+            nc.sync.dma_start(out=coef_rows[0:PASSES, :], in_=keep.rearrange("(g k) -> g k", g=PASSES))
+            nc.sync.dma_start(out=coef_rows[PASSES : 2 * PASSES, :], in_=resp.rearrange("(g k) -> g k", g=PASSES))
             issue_loads(len(step_loads(0)) + len(step_loads(1)))
             nc.sync.dma_start(out=feps_bf[:], in_=f_eps.rearrange("(p j) -> p j", j=ROW_TILES))
             issue_loads(RAW_BUFS)

@@ -24,7 +24,8 @@ PASSES = T // K_PASS
 ROW_TILES = M // P
 GROUP = 4
 WIDTH = GROUP * P
-STEPS = PASSES * ROW_TILES // GROUP
+PAIR = 2 * P
+STEPS = 2 * PASSES
 N_TILE = 512
 RUN = 4
 
@@ -58,14 +59,13 @@ def tile_continuum_reaction_field_s2_kernel(
         def tiles(name, count, shape, dtype):
             return [sb.tile(shape, dtype, name="%s%d" % (name, i), align_bytes=64) for i in range(count)]
 
-        banks = [ps.tile([P, N_TILE], F32, name="bank%d" % i) for i in range(8)]
+        banks = [ps.tile([P, N_TILE], F32, name="bank%d" % i) for i in range(2 * GROUP)]
         turn_banks, sum_banks = banks[:GROUP], banks[GROUP:]
         ident = sb.tile([P, P], F32, name="ident")
         coef_rows = sb.tile([P, K_PASS], BF16, name="coef_rows")
-        coef = sb.tile([P, 2, 4 * PASSES], F32, name="coef")
+        coef = sb.tile([P, 2, 2 * PASSES, 2], F32, name="coef")
         feps_bf = sb.tile([P, ROW_TILES], BF16, name="feps_bf")
         feps = sb.tile([P, ROW_TILES], F32, name="feps")
-        warm = sb.tile([P, 1], F32, name="warm")
         raw_bufs = tiles("raw", RAW_BUFS, [P, PACK, K_PASS], BF16)
         products = tiles("product", PRODUCT_BUFS, [P, WIDTH], F32)
         q_slots = tiles("q_slots", 2, [P, PACK, WIDTH], BF16)
@@ -77,78 +77,94 @@ def tile_continuum_reaction_field_s2_kernel(
         g_codes = {a: tiles("g_codes_" + a, 2 * PASSES, [P, N_TILE], U32) for a in green}
         g_scales = {a: tiles("g_scales_" + a, 2 * PASSES, [P, N_TILE], U8) for a in green}
 
-        taken = {"raw": 0, "turn": 0, "product": 0, "grouped": 0, "result": 0}
+        taken = {"raw": 0, "turn": 0, "product": 0, "grouped": 0, "result": 0, "ready": 0}
         raw_of, turned, product_of, grouped_of, result_of = {}, {}, {}, {}, {}
+        ready = []
 
         def take(kind, ring):
             taken[kind] = taken[kind] + 1
             return ring[(taken[kind] - 1) % len(ring)]
 
-        def load(kind, a, index):
+        def first_pass(step):
+            return 2 * (step % PASSES // 2)
+
+        def row_step(half, j, g):
+            return PASSES * half + 2 * (g // 2) + j // 2
+
+        def load(item):
+            kind, a, index = item
             raw = take("raw", raw_bufs)
-            raw_of[kind, a, index] = raw
-            half, g = divmod(index, PASSES)
-            k_range = slice(K_PASS * g, K_PASS * (g + 1))
+            raw_of[item] = raw
+            half = index // PASSES
             if kind == "rows":
-                src = rows_of[a][:, GROUP * half : GROUP * (half + 1), k_range]
+                j0, k0 = GROUP * half + 2 * (index % 2), K_PASS * first_pass(index)
+                src = rows_of[a][:, j0 : j0 + 2, k0 : k0 + 2 * K_PASS]
+                nc.sync.dma_start(out=raw[:].rearrange("p (j g) k -> p j (g k)", j=2), in_=src)
             else:
-                src = green[a][k_range, N_TILE * half : N_TILE * (half + 1)].rearrange("(p t) n -> p t n", t=PACK)
-            nc.sync.dma_start(out=raw[:], in_=src)
+                k0 = K_PASS * (index % PASSES)
+                src = green[a][k0 : k0 + K_PASS, N_TILE * half : N_TILE * (half + 1)]
+                nc.sync.dma_start(out=raw[:], in_=src.rearrange("(p t) n -> p t n", t=PACK))
 
         def every_second_word(row, u):
             return row.bitcast(F32)[:, u : K_PASS // 2 : 2]
+
+        def turn(bank, c0, a, step, jj, gg, u):
+            src = every_second_word(raw_of["rows", a, step][:, 2 * jj + gg, :], u)
+            nc.tensor.transpose(bank[:, c0 : c0 + P], src, ident[:])
 
         def turn_charges(step, u):
             for a in ("v", "q"):
                 bank = take("turn", turn_banks)
                 turned[a, step, u] = bank
-                for j in range(GROUP):
-                    src = every_second_word(raw_of["rows", a, step][:, j, :], u)
-                    nc.tensor.transpose(bank[:, P * j : P * (j + 1)], src, ident[:])
+                for gg in range(2):
+                    for jj in range(2):
+                        turn(bank, PAIR * gg + P * jj, a, step, jj, gg, u)
 
-        def turn_fields(step, pair):
+        def turn_fields(step, gg):
             bank = take("turn", turn_banks)
-            turned["e", step, pair] = bank
+            turned["e", step, gg] = bank
             for jj in range(2):
                 for u in range(2):
-                    src = every_second_word(raw_of["rows", "e", step][:, 2 * pair + jj, :], u)
-                    c0 = P * (2 * u + jj)
-                    nc.tensor.transpose(bank[:, c0 : c0 + P], src, ident[:])
+                    turn(bank, PAIR * u + P * jj, "e", step, jj, gg, u)
 
-        def half_words(bank, e):
-            return bank[:].bitcast(BF16)[:, e : 2 * WIDTH : 2]
+        def half_words(bank, gg, e):
+            return bank[:].bitcast(BF16)[:, 2 * PAIR * gg + e : 2 * PAIR * (gg + 1) : 2]
 
         def response(step, u):
             for e in range(2):
                 product = take("product", products)
                 product_of[step, u, e] = product
-                c = 2 * (PASSES + step % PASSES) + e
-                nc.scalar.activation(
-                    out=product[:], in_=half_words(turned["v", step, u], e), func=COPY, scale=coef[:, u, c : c + 1]
-                )
+                for gg in range(2):
+                    nc.scalar.activation(
+                        out=product[:, PAIR * gg : PAIR * (gg + 1)],
+                        in_=half_words(turned["v", step, u], gg, e),
+                        func=COPY,
+                        scale=coef[:, u, PASSES + first_pass(step) + gg, e : e + 1],
+                    )
 
         def charges(step, u):
             for e in range(2):
-                c = 2 * (step % PASSES) + e
-                nc.vector.scalar_tensor_tensor(
-                    out=q_slots[step % 2][:, 2 * u + e, :],
-                    in0=half_words(turned["q", step, u], e),
-                    scalar=coef[:, u, c : c + 1],
-                    in1=product_of[step, u, e][:],
-                    op0=MULT,
-                    op1=SUB,
-                )
+                for gg in range(2):
+                    cols = slice(PAIR * gg, PAIR * (gg + 1))
+                    nc.vector.scalar_tensor_tensor(
+                        out=q_slots[step % 2][:, 2 * u + e, cols],
+                        in0=half_words(turned["q", step, u], gg, e),
+                        scalar=coef[:, u, first_pass(step) + gg, e : e + 1],
+                        in1=product_of[step, u, e][:, cols],
+                        op0=MULT,
+                        op1=SUB,
+                    )
 
-        def copy_fields(step, pair):
-            if pair == 0:
+        def copy_fields(step, gg):
+            if gg == 0:
                 grouped_of["rows", "e", step] = take("grouped", grouped_bufs)
-            dst = grouped_of["rows", "e", step][:].bitcast(F32)[:, WIDTH * pair : WIDTH * (pair + 1)]
+            dst = grouped_of["rows", "e", step][:].bitcast(F32)[:, 2 * PAIR * gg : 2 * PAIR * (gg + 1)]
             nc.scalar.copy(
                 out=dst.rearrange("p (r u) -> p r u", u=2),
-                in_=turned["e", step, pair][:].rearrange("p (u r) -> p r u", u=2),
+                in_=turned["e", step, gg][:].rearrange("p (u r) -> p r u", u=2),
             )
 
-        def interleave(copy, grouped, slots, c0, c1):
+        def group(copy, grouped, slots, c0, c1):
             copy(
                 out=grouped[:, PACK * c0 : PACK * c1].rearrange("p (c i t) -> p c t i", i=RUN, t=PACK),
                 in_=slots[:, :, c0:c1].rearrange("p t (c i) -> p c t i", i=RUN),
@@ -156,7 +172,7 @@ def tile_continuum_reaction_field_s2_kernel(
 
         def group_charges(step):
             grouped_of["rows", "q", step] = take("grouped", grouped_bufs)
-            interleave(nc.vector.tensor_copy, grouped_of["rows", "q", step], q_slots[step % 2], 0, WIDTH)
+            group(nc.vector.tensor_copy, grouped_of["rows", "q", step], q_slots[step % 2], 0, WIDTH)
 
         def group_on_pool(item):
             grouped_of[item] = shared_grouped
@@ -169,6 +185,12 @@ def tile_continuum_reaction_field_s2_kernel(
                 op1=ADD,
             )
 
+        def group_on_scalar(item):
+            group(nc.scalar.copy, shared_grouped, raw_of[item], POOL_COLS, N_TILE - VECTOR_COLS)
+
+        def group_on_vector(item):
+            group(nc.vector.tensor_copy, shared_grouped, raw_of[item], N_TILE - VECTOR_COLS, N_TILE)
+
         def quantize(item):
             kind, a, index = item
             if kind == "rows":
@@ -180,12 +202,12 @@ def tile_continuum_reaction_field_s2_kernel(
         def multiply(bank, half, j, item):
             a, chunk = item[1:]
             g = chunk % PASSES
-            step = PASSES * half + g
-            cols = slice(P * j, P * (j + 1))
+            step = row_step(half, j, g)
+            c0 = PAIR * (g % 2) + P * (j % 2)
             nc.tensor.matmul_mx(
                 out=bank[:],
-                lhsT=row_codes[a][step][:, cols].bitcast(row_format[a]),
-                lhsT_scale=row_scales[a][step][:, cols],
+                lhsT=row_codes[a][step][:, c0 : c0 + P].bitcast(row_format[a]),
+                lhsT_scale=row_scales[a][step][:, c0 : c0 + P],
                 rhs=g_codes[a][chunk][:].bitcast(E4M3),
                 rhs_scale=g_scales[a][chunk][:],
                 start=(a == "q" and g == 0),
@@ -198,7 +220,16 @@ def tile_continuum_reaction_field_s2_kernel(
                     multiply(ring[j], half, j, item)
 
         def multiply_step(a, step):
-            multiply_tiles(sum_banks, step // PASSES, range(GROUP), [("g", a, step % PASSES)])
+            half = step // PASSES
+            for g in range(min(step + 1, PASSES)):
+                for j in range(GROUP):
+                    entry = (half, j, ("g", a, g))
+                    if row_step(half, j, g) <= step and entry not in ready:
+                        ready.append(entry)
+            end = len(ready) if step >= PASSES - 1 else min(len(ready), taken["ready"] + GROUP)
+            for entry_half, j, item in ready[taken["ready"] : end]:
+                multiply(sum_banks[j], entry_half, j, item)
+            taken["ready"] = end
 
         def finish(bank, half, j, n_half):
             tile_row = GROUP * half + j
@@ -216,38 +247,34 @@ def tile_continuum_reaction_field_s2_kernel(
             nc.sync.dma_start(out=dst, in_=result_of[tile_row, n_half][:])
 
         late = [("g", a, PASSES + g) for g in range(PASSES) for a in ("q", "e")]
-        window = {step: (("g", "q", step - 1), ("g", "e", step - 1)) for step in range(1, PASSES + 1)}
-        window[STEPS - 1] = (late[0], late[1])
+        chunks_of = {step: (("g", "q", step - 1), ("g", "e", step - 1)) for step in range(1, PASSES + 1)}
+        chunks_of[STEPS - 1] = (late[0], late[1])
 
         def step_loads(step):
             v_rows, q_rows, e_rows = [("rows", a, step) for a in ("v", "q", "e")]
             if 1 <= step <= PASSES:
-                return [v_rows, q_rows, window[step][0], e_rows, window[step][1]]
+                return [v_rows, q_rows, chunks_of[step][0], e_rows, chunks_of[step][1]]
             return [v_rows, q_rows, e_rows]
 
         loads = [item for step in range(STEPS) for item in step_loads(step)] + late
 
         def issue_loads(upto):
             for item in loads[taken["raw"] : upto]:
-                load(*item)
-
-        scalar_cols = (POOL_COLS, N_TILE - VECTOR_COLS)
-        vector_cols = (N_TILE - VECTOR_COLS, N_TILE)
+                load(item)
 
         with tc.manual_schedule():
             nc.vector.memset(coef_rows[:], 0.0)
             make_identity(nc, ident[:])
-            nc.scalar.activation(out=warm[:], in_=ident[:, 0:1], func=COPY)
+            nc.scalar.dma_start(out=feps_bf[:], in_=f_eps.rearrange("(p j) -> p j", j=ROW_TILES))
+            nc.scalar.activation(out=feps[:], in_=feps_bf[:], func=COPY)
             issue_loads(1)
             nc.sync.dma_start(out=coef_rows[0:PASSES, :], in_=keep.rearrange("(g k) -> g k", g=PASSES))
             nc.sync.dma_start(out=coef_rows[PASSES : 2 * PASSES, :], in_=resp.rearrange("(g k) -> g k", g=PASSES))
-            issue_loads(len(step_loads(0)) + len(step_loads(1)))
-            nc.sync.dma_start(out=feps_bf[:], in_=f_eps.rearrange("(p j) -> p j", j=ROW_TILES))
             issue_loads(RAW_BUFS)
             for u in range(2):
                 nc.tensor.transpose(sum_banks[0][:, P * u : P * (u + 1)], every_second_word(coef_rows[:], u), ident[:])
-            coef_turned = sum_banks[0][:, 0 : 2 * P].bitcast(BF16).rearrange("p (u x) -> p u x", u=2)
-            nc.vector.tensor_copy(out=coef[:], in_=coef_turned[:, :, 0 : 4 * PASSES])
+            coef_turned = sum_banks[0][:, 0:PAIR].bitcast(BF16).rearrange("p (u r e) -> p u r e", u=2, e=2)
+            nc.vector.tensor_copy(out=coef[:], in_=coef_turned[:, :, 0 : 2 * PASSES, :])
 
             freed = 0
             for step in range(STEPS):
@@ -256,28 +283,27 @@ def tile_continuum_reaction_field_s2_kernel(
                 if step >= 1:
                     turn_fields(prev, 1)
                     group_charges(prev)
-                if prev in window:
-                    quantize(window[prev][1])
+                if prev in chunks_of:
+                    quantize(chunks_of[prev][1])
                 if step >= 2:
                     multiply_step("e", step - 2)
                 response(step, 0)
-                if step in window:
-                    group_on_pool(window[step][0])
+                if step in chunks_of:
+                    group_on_pool(chunks_of[step][0])
                 charges(step, 0)
-                if step in window:
-                    interleave(nc.scalar.copy, shared_grouped, raw_of[window[step][0]], *scalar_cols)
+                if step in chunks_of:
+                    group_on_scalar(chunks_of[step][0])
                 if step >= 1:
                     copy_fields(prev, 1)
-                if step in window:
-                    interleave(nc.vector.tensor_copy, shared_grouped, raw_of[window[step][0]], *vector_cols)
+                if step in chunks_of:
+                    group_on_vector(chunks_of[step][0])
                 if step >= 1:
                     quantize(("rows", "q", prev))
                 if step - 2 == PASSES - 1:
-                    nc.vector.tensor_copy(out=feps[:], in_=feps_bf[:])
                     for j in range(GROUP):
                         finish(sum_banks[j], 0, j, 0)
-                if step in window:
-                    quantize(window[step][0])
+                if step in chunks_of:
+                    quantize(chunks_of[step][0])
 
                 turn_charges(step, 1)
                 turn_fields(step, 0)
@@ -285,14 +311,14 @@ def tile_continuum_reaction_field_s2_kernel(
                     multiply_step("q", prev)
                     quantize(("rows", "e", prev))
                 response(step, 1)
-                if step in window:
-                    group_on_pool(window[step][1])
+                if step in chunks_of:
+                    group_on_pool(chunks_of[step][1])
                 charges(step, 1)
-                if step in window:
-                    interleave(nc.scalar.copy, shared_grouped, raw_of[window[step][1]], *scalar_cols)
+                if step in chunks_of:
+                    group_on_scalar(chunks_of[step][1])
                 copy_fields(step, 0)
-                if step in window:
-                    interleave(nc.vector.tensor_copy, shared_grouped, raw_of[window[step][1]], *vector_cols)
+                if step in chunks_of:
+                    group_on_vector(chunks_of[step][1])
                 if step >= 1:
                     freed = freed + len(step_loads(prev))
                     issue_loads(RAW_BUFS + freed)
@@ -300,39 +326,42 @@ def tile_continuum_reaction_field_s2_kernel(
                 store(0, j, 0)
 
             last = STEPS - 1
+            early = len(chunks_of[last])
             turn_fields(last, 1)
             group_charges(last)
             multiply_step("e", last - 1)
             copy_fields(last, 1)
-            quantize(late[1])
-            quantize(("rows", "q", last))
+            quantize(chunks_of[last][1])
             quantize(("rows", "e", last))
+            quantize(("rows", "q", last))
             free_banks = [turn_banks[(taken["turn"] + i) % GROUP] for i in range(GROUP)]
-            multiply_tiles(free_banks, 0, range(GROUP // 2), late[:2])
+            for item in late[:early]:
+                multiply_tiles(free_banks, 0, range(GROUP - 1), [item])
+            multiply_tiles(free_banks, 0, [GROUP - 1], late[:early])
             multiply_step("q", last)
             multiply_step("e", last)
-            multiply_tiles(free_banks, 0, range(GROUP // 2, GROUP), late[:2])
 
-            for i in range(2, len(late) + 1):
+            for i in range(early, len(late) + 1):
                 if i < len(late):
                     grouped_of[late[i]] = take("grouped", grouped_bufs)
                     split = N_TILE - VECTOR_COLS_END
-                    interleave(nc.scalar.copy, grouped_of[late[i]], raw_of[late[i]], 0, split)
-                    interleave(nc.vector.tensor_copy, grouped_of[late[i]], raw_of[late[i]], split, N_TILE)
-                if i > 2:
+                    group(nc.scalar.copy, grouped_of[late[i]], raw_of[late[i]], 0, split)
+                    group(nc.vector.tensor_copy, grouped_of[late[i]], raw_of[late[i]], split, N_TILE)
+                if i > early:
                     quantize(late[i - 1])
-                if i == 3:
+                if i == early + 1:
                     for j in range(GROUP):
                         finish(sum_banks[j], 1, j, 0)
                         store(1, j, 0)
 
             shared = len(late) - END_CHUNKS
             behind = 0
-            for i in range(2, shared):
+            for i in range(early, shared):
                 multiply_tiles(free_banks, 0, range(GROUP), [late[i]])
                 upto = min(behind + 2, i + 1)
                 multiply_tiles(sum_banks, 1, range(GROUP), late[behind:upto])
                 behind = upto
+            assert behind == shared
             for half, ring in enumerate((free_banks, sum_banks)):
                 for j in range(GROUP):
                     multiply_tiles(ring, half, [j], late[shared:])

from contextlib import ExitStack

import concourse.mybir as mybir
from concourse.masks import make_identity

M, T, N = 1024, 2048, 1024
FLOPS = 2 * 2 * M * T * N

F32 = mybir.dt.float32
BF16 = mybir.dt.bfloat16
U32 = mybir.dt.uint32
U8 = mybir.dt.uint8
E4M3 = mybir.dt.float8_e4m3fn_x4
E5M2 = mybir.dt.float8_e5m2_x4
COPY = mybir.ActivationFunctionType.Copy
MULT = mybir.AluOpType.mult
SUB = mybir.AluOpType.subtract
ADD = mybir.AluOpType.add

P = 128
PACK = 4
K_PASS = P * PACK
PASSES = T // K_PASS
ROW_TILES = M // P
GROUP = 4
WIDTH = GROUP * P
PAIR = 2 * P
STEPS = 2 * PASSES
N_TILE = 512
RUN = 4

RAW_BUFS = 24
PRODUCT_BUFS = 4
GROUPED_BUFS = 5
RESULT_BUFS = 6
POOL_COLS = 160
VECTOR_COLS = 64
VECTOR_COLS_END = 288
END_CHUNKS = 3


def tile_continuum_reaction_field_s2_kernel(
    tc, v, q_old, keep, resp, e_norm, g_single, g_double, f_eps, out
):
    nc = tc.nc
    rows_of = {
        "v": v.rearrange("(p j) k -> p j k", j=ROW_TILES),
        "q": q_old.rearrange("(p j) k -> p j k", j=ROW_TILES),
        "e": e_norm.rearrange("(p j) k -> p j k", j=ROW_TILES),
    }
    green = {"q": g_single, "e": g_double}
    row_format = {"q": E4M3, "e": E5M2}
    out_rows = out.rearrange("(p j) n -> p j n", j=ROW_TILES)

    with ExitStack() as ctx:
        sb = ctx.enter_context(tc.tile_pool(name="sb", bufs=1))
        ps = ctx.enter_context(tc.psum_pool(name="ps", bufs=1))

        def tiles(name, count, shape, dtype):
            return [sb.tile(shape, dtype, name="%s%d" % (name, i), align_bytes=64) for i in range(count)]

        banks = [ps.tile([P, N_TILE], F32, name="bank%d" % i) for i in range(2 * GROUP)]
        turn_banks, sum_banks = banks[:GROUP], banks[GROUP:]
        ident = sb.tile([P, P], F32, name="ident")
        coef_rows = sb.tile([P, K_PASS], BF16, name="coef_rows")
        coef = sb.tile([P, 2, 2 * PASSES, 2], F32, name="coef")
        feps_bf = sb.tile([P, ROW_TILES], BF16, name="feps_bf")
        feps = sb.tile([P, ROW_TILES], F32, name="feps")
        raw_bufs = tiles("raw", RAW_BUFS, [P, PACK, K_PASS], BF16)
        products = tiles("product", PRODUCT_BUFS, [P, WIDTH], F32)
        q_slots = tiles("q_slots", 2, [P, PACK, WIDTH], BF16)
        grouped_bufs = tiles("grouped", GROUPED_BUFS, [P, PACK * WIDTH], BF16)
        shared_grouped = sb.tile([P, PACK * N_TILE], BF16, name="shared_grouped", align_bytes=64)
        results = tiles("result", RESULT_BUFS, [P, N_TILE], F32)
        row_codes = {a: tiles("row_codes_" + a, STEPS, [P, WIDTH], U32) for a in green}
        row_scales = {a: tiles("row_scales_" + a, STEPS, [P, WIDTH], U8) for a in green}
        g_codes = {a: tiles("g_codes_" + a, 2 * PASSES, [P, N_TILE], U32) for a in green}
        g_scales = {a: tiles("g_scales_" + a, 2 * PASSES, [P, N_TILE], U8) for a in green}

        taken = {"raw": 0, "turn": 0, "product": 0, "grouped": 0, "result": 0, "ready": 0}
        raw_of, turned, product_of, grouped_of, result_of = {}, {}, {}, {}, {}
        ready = []

        def take(kind, ring):
            taken[kind] = taken[kind] + 1
            return ring[(taken[kind] - 1) % len(ring)]

        def first_pass(step):
            return 2 * (step % PASSES // 2)

        def row_step(half, j, g):
            return PASSES * half + 2 * (g // 2) + j // 2

        def load(item):
            kind, a, index = item
            raw = take("raw", raw_bufs)
            raw_of[item] = raw
            half = index // PASSES
            if kind == "rows":
                j0, k0 = GROUP * half + 2 * (index % 2), K_PASS * first_pass(index)
                src = rows_of[a][:, j0 : j0 + 2, k0 : k0 + 2 * K_PASS]
                nc.sync.dma_start(out=raw[:].rearrange("p (j g) k -> p j (g k)", j=2), in_=src)
            else:
                k0 = K_PASS * (index % PASSES)
                src = green[a][k0 : k0 + K_PASS, N_TILE * half : N_TILE * (half + 1)]
                nc.sync.dma_start(out=raw[:], in_=src.rearrange("(p t) n -> p t n", t=PACK))

        def every_second_word(row, u):
            return row.bitcast(F32)[:, u : K_PASS // 2 : 2]

        def turn(bank, c0, a, step, jj, gg, u):
            src = every_second_word(raw_of["rows", a, step][:, 2 * jj + gg, :], u)
            nc.tensor.transpose(bank[:, c0 : c0 + P], src, ident[:])

        def turn_charges(step, u):
            for a in ("v", "q"):
                bank = take("turn", turn_banks)
                turned[a, step, u] = bank
                for gg in range(2):
                    for jj in range(2):
                        turn(bank, PAIR * gg + P * jj, a, step, jj, gg, u)

        def turn_fields(step, gg):
            bank = take("turn", turn_banks)
            turned["e", step, gg] = bank
            for jj in range(2):
                for u in range(2):
                    turn(bank, PAIR * u + P * jj, "e", step, jj, gg, u)

        def half_words(bank, gg, e):
            return bank[:].bitcast(BF16)[:, 2 * PAIR * gg + e : 2 * PAIR * (gg + 1) : 2]

        def response(step, u):
            for e in range(2):
                product = take("product", products)
                product_of[step, u, e] = product
                for gg in range(2):
                    nc.scalar.activation(
                        out=product[:, PAIR * gg : PAIR * (gg + 1)],
                        in_=half_words(turned["v", step, u], gg, e),
                        func=COPY,
                        scale=coef[:, u, PASSES + first_pass(step) + gg, e : e + 1],
                    )

        def charges(step, u):
            for e in range(2):
                for gg in range(2):
                    cols = slice(PAIR * gg, PAIR * (gg + 1))
                    nc.vector.scalar_tensor_tensor(
                        out=q_slots[step % 2][:, 2 * u + e, cols],
                        in0=half_words(turned["q", step, u], gg, e),
                        scalar=coef[:, u, first_pass(step) + gg, e : e + 1],
                        in1=product_of[step, u, e][:, cols],
                        op0=MULT,
                        op1=SUB,
                    )

        def copy_fields(step, gg):
            if gg == 0:
                grouped_of["rows", "e", step] = take("grouped", grouped_bufs)
            dst = grouped_of["rows", "e", step][:].bitcast(F32)[:, 2 * PAIR * gg : 2 * PAIR * (gg + 1)]
            nc.scalar.copy(
                out=dst.rearrange("p (r u) -> p r u", u=2),
                in_=turned["e", step, gg][:].rearrange("p (u r) -> p r u", u=2),
            )

        def group(copy, grouped, slots, c0, c1):
            copy(
                out=grouped[:, PACK * c0 : PACK * c1].rearrange("p (c i t) -> p c t i", i=RUN, t=PACK),
                in_=slots[:, :, c0:c1].rearrange("p t (c i) -> p c t i", i=RUN),
            )

        def group_charges(step):
            grouped_of["rows", "q", step] = take("grouped", grouped_bufs)
            group(nc.vector.tensor_copy, grouped_of["rows", "q", step], q_slots[step % 2], 0, WIDTH)

        def group_on_pool(item):
            grouped_of[item] = shared_grouped
            nc.gpsimd.tensor_scalar(
                out=shared_grouped[:, 0 : PACK * POOL_COLS].rearrange("p (c t) -> p c t", t=PACK),
                in0=raw_of[item][:, :, 0:POOL_COLS].rearrange("p t c -> p c t"),
                scalar1=1.0,
                scalar2=0.0,
                op0=MULT,
                op1=ADD,
            )

        def group_on_scalar(item):
            group(nc.scalar.copy, shared_grouped, raw_of[item], POOL_COLS, N_TILE - VECTOR_COLS)

        def group_on_vector(item):
            group(nc.vector.tensor_copy, shared_grouped, raw_of[item], N_TILE - VECTOR_COLS, N_TILE)

        def quantize(item):
            kind, a, index = item
            if kind == "rows":
                codes, scales = row_codes[a][index][:].bitcast(row_format[a]), row_scales[a][index]
            else:
                codes, scales = g_codes[a][index][:].bitcast(E4M3), g_scales[a][index]
            nc.vector.quantize_mx(out=codes, scales=scales[:], in_=grouped_of[item][:])

        def multiply(bank, half, j, item):
            a, chunk = item[1:]
            g = chunk % PASSES
            step = row_step(half, j, g)
            c0 = PAIR * (g % 2) + P * (j % 2)
            nc.tensor.matmul_mx(
                out=bank[:],
                lhsT=row_codes[a][step][:, c0 : c0 + P].bitcast(row_format[a]),
                lhsT_scale=row_scales[a][step][:, c0 : c0 + P],
                rhs=g_codes[a][chunk][:].bitcast(E4M3),
                rhs_scale=g_scales[a][chunk][:],
                start=(a == "q" and g == 0),
                stop=(a == "e" and g == PASSES - 1),
            )

        def multiply_tiles(ring, half, tile_range, items):
            for j in tile_range:
                for item in items:
                    multiply(ring[j], half, j, item)

        def multiply_step(a, step):
            half = step // PASSES
            for g in range(min(step + 1, PASSES)):
                for j in range(GROUP):
                    entry = (half, j, ("g", a, g))
                    if row_step(half, j, g) <= step and entry not in ready:
                        ready.append(entry)
            end = len(ready) if step >= PASSES - 1 else min(len(ready), taken["ready"] + GROUP)
            for entry_half, j, item in ready[taken["ready"] : end]:
                multiply(sum_banks[j], entry_half, j, item)
            taken["ready"] = end

        def finish(bank, half, j, n_half):
            tile_row = GROUP * half + j
            result = take("result", results)
            result_of[tile_row, n_half] = result
            factor = feps[:, tile_row : tile_row + 1]
            if j % 2 == 0:
                nc.scalar.activation(out=result[:], in_=bank[:], func=COPY, scale=factor)
            else:
                nc.vector.tensor_scalar(out=result[:], in0=bank[:], scalar1=factor, scalar2=None, op0=MULT)

        def store(half, j, n_half):
            tile_row = GROUP * half + j
            dst = out_rows[:, tile_row, N_TILE * n_half : N_TILE * (n_half + 1)]
            nc.sync.dma_start(out=dst, in_=result_of[tile_row, n_half][:])

        late = [("g", a, PASSES + g) for g in range(PASSES) for a in ("q", "e")]
        chunks_of = {step: (("g", "q", step - 1), ("g", "e", step - 1)) for step in range(1, PASSES + 1)}
        chunks_of[STEPS - 1] = (late[0], late[1])

        def step_loads(step):
            v_rows, q_rows, e_rows = [("rows", a, step) for a in ("v", "q", "e")]
            if 1 <= step <= PASSES:
                return [v_rows, q_rows, chunks_of[step][0], e_rows, chunks_of[step][1]]
            return [v_rows, q_rows, e_rows]

        loads = [item for step in range(STEPS) for item in step_loads(step)] + late

        def issue_loads(upto):
            for item in loads[taken["raw"] : upto]:
                load(item)

        with tc.manual_schedule():
            nc.vector.memset(coef_rows[:], 0.0)
            make_identity(nc, ident[:])
            nc.scalar.dma_start(out=feps_bf[:], in_=f_eps.rearrange("(p j) -> p j", j=ROW_TILES))
            nc.scalar.activation(out=feps[:], in_=feps_bf[:], func=COPY)
            issue_loads(1)
            nc.sync.dma_start(out=coef_rows[0:PASSES, :], in_=keep.rearrange("(g k) -> g k", g=PASSES))
            nc.sync.dma_start(out=coef_rows[PASSES : 2 * PASSES, :], in_=resp.rearrange("(g k) -> g k", g=PASSES))
            issue_loads(RAW_BUFS)
            for u in range(2):
                nc.tensor.transpose(sum_banks[0][:, P * u : P * (u + 1)], every_second_word(coef_rows[:], u), ident[:])
            coef_turned = sum_banks[0][:, 0:PAIR].bitcast(BF16).rearrange("p (u r e) -> p u r e", u=2, e=2)
            nc.vector.tensor_copy(out=coef[:], in_=coef_turned[:, :, 0 : 2 * PASSES, :])

            freed = 0
            for step in range(STEPS):
                prev = step - 1
                turn_charges(step, 0)
                if step >= 1:
                    turn_fields(prev, 1)
                    group_charges(prev)
                if prev in chunks_of:
                    quantize(chunks_of[prev][1])
                if step >= 2:
                    multiply_step("e", step - 2)
                response(step, 0)
                if step in chunks_of:
                    group_on_pool(chunks_of[step][0])
                charges(step, 0)
                if step in chunks_of:
                    group_on_scalar(chunks_of[step][0])
                if step >= 1:
                    copy_fields(prev, 1)
                if step in chunks_of:
                    group_on_vector(chunks_of[step][0])
                if step >= 1:
                    quantize(("rows", "q", prev))
                if step - 2 == PASSES - 1:
                    for j in range(GROUP):
                        finish(sum_banks[j], 0, j, 0)
                if step in chunks_of:
                    quantize(chunks_of[step][0])

                turn_charges(step, 1)
                turn_fields(step, 0)
                if step >= 1:
                    multiply_step("q", prev)
                    quantize(("rows", "e", prev))
                response(step, 1)
                if step in chunks_of:
                    group_on_pool(chunks_of[step][1])
                charges(step, 1)
                if step in chunks_of:
                    group_on_scalar(chunks_of[step][1])
                copy_fields(step, 0)
                if step in chunks_of:
                    group_on_vector(chunks_of[step][1])
                if step >= 1:
                    freed = freed + len(step_loads(prev))
                    issue_loads(RAW_BUFS + freed)
            for j in range(GROUP):
                store(0, j, 0)

            last = STEPS - 1
            early = len(chunks_of[last])
            turn_fields(last, 1)
            group_charges(last)
            multiply_step("e", last - 1)
            copy_fields(last, 1)
            quantize(chunks_of[last][1])
            quantize(("rows", "e", last))
            quantize(("rows", "q", last))
            free_banks = [turn_banks[(taken["turn"] + i) % GROUP] for i in range(GROUP)]
            for item in late[:early]:
                multiply_tiles(free_banks, 0, range(GROUP - 1), [item])
            multiply_tiles(free_banks, 0, [GROUP - 1], late[:early])
            multiply_step("q", last)
            multiply_step("e", last)

            for i in range(early, len(late) + 1):
                if i < len(late):
                    grouped_of[late[i]] = take("grouped", grouped_bufs)
                    split = N_TILE - VECTOR_COLS_END
                    group(nc.scalar.copy, grouped_of[late[i]], raw_of[late[i]], 0, split)
                    group(nc.vector.tensor_copy, grouped_of[late[i]], raw_of[late[i]], split, N_TILE)
                if i > early:
                    quantize(late[i - 1])
                if i == early + 1:
                    for j in range(GROUP):
                        finish(sum_banks[j], 1, j, 0)
                        store(1, j, 0)

            shared = len(late) - END_CHUNKS
            behind = 0
            for i in range(early, shared):
                multiply_tiles(free_banks, 0, range(GROUP), [late[i]])
                upto = min(behind + 2, i + 1)
                multiply_tiles(sum_banks, 1, range(GROUP), late[behind:upto])
                behind = upto
            assert behind == shared
            for half, ring in enumerate((free_banks, sum_banks)):
                for j in range(GROUP):
                    multiply_tiles(ring, half, [j], late[shared:])
                    finish(ring[j], half, j, 1)
                    store(half, j, 1)
